import numpy as np, ml_dtypes
CORES = [40,64,80,88,96,104,120,144]
N = 8
BF = ml_dtypes.bfloat16
def gentries(a):
    return np.ascontiguousarray(a.reshape(8, 16, -1).transpose(0, 2, 1)).reshape(8, -1)
def gtable(e):
    e = np.asarray(e); return np.ascontiguousarray(e.reshape(8, -1, 16).transpose(0, 2, 1)).reshape(128, -1).astype(np.int32)
D, W, H, B, T = 1280, 1792, 4, 1, 1024
M = H * B
TOP = np.arange(16)[:, None]
def counts(rng, n):
    return np.minimum(M + ((96 - M) * rng.random((N, 8, 16, n)) ** rng.choice(np.array([1.0, 2.0, 4.0]), (N, 8, 1, n))).astype(np.int64), 95)
def lists(rng, n):
    return np.ascontiguousarray(np.argsort(rng.random((N, 8, M, n)), axis=-1)[..., :T])
def parts(rng):
    return (counts(rng, D), counts(rng, W), rng.integers(1, 4, (N, 8, 16, H)), lists(rng, D), lists(rng, W), rng.integers(0, 16, (N, 8, M, T)), rng.integers(0, 32, (N, 8, M, T)))
def near(p):
    t = p[:, :, 15:]; a = 32 * p[:, :, :15]; v = a // t; i = np.argmin(a - v * t, axis=2)[:, :, None]
    return np.take_along_axis(v, i, 2)[:, :, 0]
def pack(cd, cw, wt, dl, wl, zo, dr):
    b = lambda a, p: np.ascontiguousarray(a).reshape(N, p, -1).astype(np.float32).astype(BF)
    return {"nd": b(cd, 128), "nw": b(cw, 128), "wt": np.ascontiguousarray(wt).reshape(N, 128, H).astype(np.float32),
            "dl": np.stack([gtable(a.reshape(8, -1)) for a in dl]), "wl": np.stack([gtable(a.reshape(8, -1)) for a in wl]), "zo": b(zo, 8), "dr": b(dr, 8)}
def setup_inputs(rng):
    return pack(*parts(rng))
def setup_inputs_drain(rng):
    cd, cw, wt, dl, wl, zo, dr = parts(rng); s = (N, 8, M, T)
    u = np.argsort(rng.random((8, W)), axis=-1)[:, :T]; q = np.argsort(rng.random((N, 8, D)), axis=-1)[..., :T]; zeta = rng.integers(1, 16, (8, T))
    o = np.argsort(rng.random(s), axis=-1)
    dl = np.take_along_axis(np.broadcast_to(q[:, :, None], s), o, 3); wl = np.take_along_axis(np.broadcast_to(u[None, :, None], s), o, 3); zo = np.take_along_axis(np.broadcast_to(zeta[None, :, None], s), o, 3)
    dr[:, ::2] = 0
    for c, n in ((cd, D), (cw, W)):
        k = rng.integers(0, 4, (N, 4, 1, n))
        c[:, ::2] = np.where(k == 3, M + rng.integers(0, 2, (N, 4, 16, n)), np.where(k == 2, M, np.where(TOP == 0, 95, np.where(k == 0, M, c[:, ::2]))))
    i = dl[:, ::2, M - 1][:, :, None, :]; j = wl[:, ::2, M - 1][:, :, None, :]; z = zo[:, ::2, M - 1][:, :, None, :]
    more = 1 + (M - 1) * (TOP == 0) - M * (TOP == z)
    x = np.take_along_axis(cd[:, ::2], i, 3) + more; y = np.take_along_axis(cw[(np.arange(N) + H - 1) % N][:, ::2], j, 3) + more
    p = np.add.accumulate(x * y * wt[:, ::2, :, H - 1][..., None], axis=2)
    dr[:, ::2, M - 1] = np.where(rng.random((N, 4, T)) < 0.5, near(p), 0)
    return pack(cd, cw, wt, dl, wl, zo, dr)
def setup_inputs_ends(rng):
    cd, cw, wt, dl, wl, zo, dr = parts(rng)
    cd[:, 0] = 95; cw[:, 0] = 95; wt[:, 0] = 3; cd[:, 1] = M; cw[:, 1] = M; wt[:, 1] = 1
    dl[:, 2] = np.arange(T); wl[:, 2] = np.arange(W - T, W); dl[:, 3] = np.arange(D - 1, D - T - 1, -1); wl[:, 3] = np.arange(T - 1, -1, -1)
    dl[:, 4] = dl[:, 4, :1].copy(); wl[:, 4] = wl[:1, 4, :1].copy()
    for a, n in ((dl, D), (wl, W)):
        a[:, 5, :, 0] = (n - 1) * (np.arange(M) % 2); a[:, 5, :, T - 1] = (n - 1) * ((np.arange(M) + 1) % 2)
        a[:, 5, :, 1:T - 1] = 1 + np.argsort(rng.random((N, M, n - 2)), axis=-1)[..., :T - 2]
    zo[:, 1:4] = 15 * rng.integers(0, 2, (N, 3, M, T)); dr[:, 1:5] = 31 * rng.integers(0, 2, (N, 4, M, T))
    return pack(cd, cw, wt, dl, wl, zo, dr)
def setup_inputs_spread(rng):
    cd, cw, wt, dl, wl, zo, dr = parts(rng)
    cd, cw = [np.minimum(M + (np.exp2(7 * rng.random((N, 8, 1, n))) * rng.random((N, 8, 16, n))).astype(np.int64), 95) for n in (D, W)]
    wt = np.where(rng.random((N, 8, 16, H)) < rng.random((N, 8, 1, 1)), 1, wt)
    zo = np.minimum((16 * rng.random((N, 8, M, T)) ** np.exp2(rng.integers(-2, 3, (N, 8, M, 1)))).astype(np.int64), 15)
    dr = np.minimum((32 * rng.random((N, 8, M, T)) ** np.exp2(rng.integers(-2, 3, (N, 8, M, 1)))).astype(np.int64), 31)
    return pack(cd, cw, wt, dl, wl, zo, dr)
def setup_inputs_ties(rng):
    cd, cw, wt, dl, wl, zo, dr = parts(rng)
    zeta = rng.integers(0, 16, (1, 8, 1, 1)); up = (TOP == zeta).astype(np.int64)
    cd = rng.integers(M, 95, (N, 8, 1, D)) + up; cw = rng.integers(M, 95, (N, 8, 1, W)) + up
    wt = np.broadcast_to(rng.integers(1, 4, (N, 8, 1, H)), (N, 8, 16, H)); zo = np.broadcast_to(zeta, (N, 8, M, T))
    return pack(cd, cw, wt, dl, wl, zo, dr)
def setup_inputs_gaps(rng):
    cd, cw, wt, dl, wl, zo, dr = parts(rng); s = (N, 3, T)
    a = np.zeros((N, 3, 16, T), np.int64); b = np.zeros((N, 3, 16, T), np.int64)
    a[:, :, 15] = rng.integers(50, 55, s); b[:, :, 15] = rng.integers(50, 55, s)
    goal = 93 * a[:, :, 15] * b[:, :, 15] + rng.integers(-1, 2, s)
    sa = np.zeros((N, 3, 15, T), np.int64); sb = np.zeros((N, 3, 15, T), np.int64); rest = (goal - 7848) // 3
    for k in range(13):
        left = 13 - k; c = rng.integers(75, 96, s); n = (2 * rest + left * c) // (2 * left * c) if k < 12 else rest // c
        if k == 0: c, n = np.full(s, 95), np.full(s, 91)
        sa[:, :, k] = n; sb[:, :, k] = c; rest = rest - n * c
    rem = 7848 + (goal - 7848) % 3 + 3 * rest
    t = rem % 80; t = np.where(t < 9, t + 80, t)
    sa[:, :, 13] = t; sb[:, :, 13] = 81; sa[:, :, 14] = (rem - 81 * t) // 80; sb[:, :, 14] = 80
    flip = rng.random((N, 3, 1, T)) < 0.5; sa, sb = np.where(flip, sb, sa), np.where(flip, sa, sb)
    od = np.argsort(rng.random((N, 3, 15)), axis=-1); ix = np.broadcast_to(od[..., None], (N, 3, 15, T))
    np.put_along_axis(a, ix, sa, 2); np.put_along_axis(b, ix, sb, 2)
    wv = np.full((N, 3, 16), 3); np.put_along_axis(wv, od[..., 13:], 1, 2); wt[:, :3, :, 0] = wv
    up = (TOP == zo[:, :3, 0][:, :, None, :]).astype(np.int64)
    np.put_along_axis(cd[:, :3], dl[:, :3, 0][:, :, None, :], a - 1 + up, 3); np.put_along_axis(cw[:, :3], wl[:, :3, 0][:, :, None, :], b - 1 + up, 3)
    dr[:, :3, 0] = np.where(rng.random(s) < 0.75, 31, dr[:, :3, 0])
    o = np.argsort(rng.random((N, 2, M, T)), axis=-1)
    dl[:, 3:5] = o; wl[:, 3:5] = o - o % 16 + (5 * o + 3) % 16
    dl[:, 4] = D - 1 - dl[:, 4]; wl[:, 4] = W - 1 - wl[:, 4]
    for c, n in ((dl, D), (wl, W)):
        k = rng.random((N, 2, M, n)) - 2 * (np.arange(n) % 16 == rng.integers(0, 16, (N, 2, M, 1)))
        i = np.argsort(k, axis=-1)[..., :T]
        c[:, 5:7] = np.take_along_axis(i, np.argsort(rng.random(i.shape), axis=-1), 3)
    return pack(cd, cw, wt, dl, wl, zo, dr)
def check_inputs(d):
    bad = []
    for k, lo, hi in (("nd", M, 95), ("nw", M, 95), ("wt", 1, 3), ("dl", 0, D - 1), ("wl", 0, W - 1), ("zo", 0, 15), ("dr", 0, 31)):
        a = np.asarray(d[k]).astype(np.float64)
        if not (np.min(a) >= lo and np.max(a) <= hi): bad.append("range of " + k)
        if np.any(a != np.floor(a)): bad.append("whole numbers in " + k)
    for k in ("dl", "wl"):
        s = np.sort(np.stack([gentries(a) for a in d[k]]).reshape(N, 8, M, T), axis=-1)
        if np.any(s[..., 1:] == s[..., :-1]): bad.append("different numbers in a batch of " + k)
    return bad
def reference(nd, nw, wt, dl, wl, zo, dr):
    whole = lambda a: a.astype(np.float32).astype(np.int64)
    docs = whole(nd).reshape(N, 8, 16, D); blocks = whole(nw).reshape(N, 8, 16, W); weight = whole(wt).reshape(N, 8, 16, H)
    dls = np.stack([gentries(a) for a in dl]).astype(np.int64).reshape(N, 8, M, T); wls = np.stack([gentries(a) for a in wl]).astype(np.int64).reshape(N, 8, M, T)
    olds = whole(zo).reshape(N, 8, M, T); draws = whole(dr).reshape(N, 8, M, T); news = np.zeros((N, 8, M, T), np.int64)
    for h in range(H):
        who = (np.arange(N) + h) % N; mine = blocks[who]
        for b in range(B):
            m = h * B + b; di = dls[:, :, m][:, :, None, :]; wi = wls[:, :, m][:, :, None, :]
            old = (olds[:, :, m][:, :, None, :] == TOP).astype(np.int64)
            x = np.take_along_axis(docs, di, 3) - old; y = np.take_along_axis(mine, wi, 3) - old
            p = np.add.accumulate((x + 1) * (y + 1) * weight[:, :, :, h][..., None], axis=2)
            z = np.add.reduce((32 * p <= draws[:, :, m][:, :, None, :] * p[:, :, 15:]).astype(np.int64), axis=2)
            new = (z[:, :, None, :] == TOP).astype(np.int64)
            np.put_along_axis(docs, di, x + new, 3); np.put_along_axis(mine, wi, y + new, 3)
            news[:, :, m] = z
        blocks[who] = mine
    last = blocks[(np.arange(N) + H - 1) % N]
    return {"yd": docs.reshape(N, 128, D).astype(np.float32).astype(BF), "yw": last.reshape(N, 128, W).astype(np.float32).astype(BF), "yz": news.reshape(N, 8, M * T).astype(np.float32).astype(BF)}

from concourse.bass import DstId, RemoteDMATransfer
from concourse.mybir import AluOpType, ActivationFunctionType

D, W, H, TK = 1280, 1792, 4, 1024
K = 48.0
CH = [(0, 128), (128, 384), (384, 640), (640, 896), (896, 1024)]
NC = len(CH)
NBV = {2, 3, 4}
NBL = {3, 4}
DOCP = [(0, 256), (256, 512), (512, 768), (768, 1024)]
DOC = 128
CUT = 896
EST = {"cy": 1.04e-3, "pe": 0.52e-3, "g": 1.56, "s": 3.8, "fix": 0.06, "sem": 0.09, "call": 0.5,
       "chunk": 4.6, "table": 6.5}
ORDER = [
    0, 1, 2, 3, 4, 5, 6, 7, 8, 9, 10, 15, 11, 17, 13, 16, 19, 33, 23, 26, 14, 27, 22, 12, 20, 21, 18, 24, 48, 37, 58, 55,
    25, 34, 43, 45, 49, 38, 61, 59, 39, 64, 65, 50, 56, 57, 62, 28, 29, 32, 35, 31, 30, 36, 51, 44, 60, 123, 63, 124, 71,
    77, 82, 72, 83, 54, 73, 66, 84, 93, 74, 94, 103, 95, 104, 85, 75, 86, 76, 53, 67, 78, 79, 80, 96, 87, 40, 68, 81, 88,
    89, 113, 125, 52, 90, 105, 126, 97, 98, 106, 127, 114, 99, 91, 46, 115, 107, 100, 116, 108, 117, 42, 109, 118, 152,
    101, 41, 110, 129, 119, 92, 128, 111, 102, 120, 130, 121, 131, 132, 135, 136, 137, 133, 138, 134, 139, 112, 153, 122,
    159, 155, 147, 148, 141, 142, 156, 143, 144, 157, 149, 154, 69, 150, 151, 166, 140, 145, 146, 162, 177, 158, 160,
    218, 219, 161, 172, 164, 167, 163, 178, 168, 179, 169, 188, 189, 180, 170, 171, 181, 208, 173, 174, 190, 191, 70,
    183, 182, 184, 185, 198, 199, 209, 192, 193, 165, 220, 201, 175, 200, 194, 186, 221, 210, 195, 222, 202, 203, 211,
    196, 212, 176, 213, 204, 224, 225, 205, 206, 226, 214, 215, 223, 247, 248, 187, 197, 242, 243, 227, 230, 228, 231,
    232, 233, 249, 236, 237, 250, 251, 229, 207, 47, 238, 252, 216, 234, 257, 244, 245, 254, 239, 217, 246, 261, 235,
    240, 241, 253, 313, 255, 262, 256, 314, 267, 272, 263, 273, 258, 274, 264, 265, 275, 266, 268, 283, 284, 285, 269,
    276, 277, 293, 278, 294, 259, 303, 270, 286, 295, 260, 279, 280, 281, 304, 287, 288, 305, 315, 316, 317, 296, 289,
    297, 306, 290, 298, 319, 299, 300, 318, 307, 308, 291, 271, 282, 320, 321, 292, 309, 310, 337, 301, 355, 356, 322,
    325, 326, 327, 328, 311, 302, 358, 342, 331, 332, 333, 323, 359, 338, 324, 329, 330, 339, 343, 344, 345, 346, 347,
    348, 349, 350, 351, 352, 353, 354, 360, 312, 340, 362, 357, 334, 335, 341, 336, 361, 410, 411, 363, 367, 365, 373,
    376, 368, 377, 364, 366, 370, 379, 369, 371, 372, 378, 380, 385, 374, 386, 388, 381, 412, 375, 382, 387, 389, 383,
    413, 416, 414, 417, 390, 394, 395, 397, 384, 415, 418, 391, 402, 403, 419, 392, 393, 396, 398, 404, 422, 434, 399,
    423, 420, 400, 421, 424, 425, 405, 406, 407, 435, 426, 436, 439, 401, 408, 428, 427, 437, 429, 430, 409, 438, 445,
    440, 441, 442, 443, 444, 431, 432, 433, 448, 449, 446, 447]

BF, F32 = "bfloat16", "float32"
SCRATCH = {"wn16": ("sbuf", [128, 192], "uint16"), "em": ("sbuf", [8, 128], BF),
           "z8": ("sbuf", [8, 4 * TK], BF), "v8": ("sbuf", [8, 4 * TK], BF)}
for _names, _where, _cols, _dt in (
        ("tab0 tab1 tab2 tab3", "sbuf", W, BF), ("nbo sg", "sbuf", 4 * TK, BF), ("nbi", "sbuf", 3 * TK, BF),
        ("ndb", "sbuf", D, BF), ("at", "sbuf", D, F32), ("dl32 wl32", "sbuf", 256, "int32"),
        ("dl16 wl16", "sbuf", 256, "uint16"), ("wts col", "sbuf", 4, F32), ("ne yb xg", "sbuf", TK, BF),
        ("ww wv na", "sbuf", TK, F32), ("zc", "sbuf", 256, BF), ("gm rr nbd l32 t1 t2 t3 t4", "sbuf", 128, F32),
        ("pci", "sbuf", 1, "int32"), ("pcf", "sbuf", 1, F32), ("gii", "sbuf", 2, "int32"), ("gif", "sbuf", 2, F32),
        ("idm m1 dm dm2", "sbuf", 128, BF), ("um", "sbuf", 144, BF), ("lw jw", "sbuf", 512, F32),
        ("px pv", "psum", TK, F32), ("pq0 pq1 pn0 pa", "psum", 512, F32)):
    for _n in _names.split():
        SCRATCH[_n] = (_where, [128, _cols], _dt)
LOADS = ["wla", "wlb", "dla", "dlb", "za", "zb", "va", "vb", "nwl", "ndl", "wtl", "oyd0", "oyd1", "oyw", "oyz"]
SEMAPHORES = (["pe", "act", "dve", "pool", "sent", "lsa", "lsb"] + LOADS + ["tb%d" % h for h in range(3)]
              + ["ck%d_%d" % (h, c) for h in range(3) for c in range(NC)])

ALU = AluOpType
ACT = ActivationFunctionType


def _mask(engines):
    m = 0
    for e in engines:
        m |= 1 << e
    return m


def _relays(src, dst, topo):
    ok = [c for c in topo.cores_of(src) if c != src and topo.may_write(c, dst)]
    near = [c for c in ok if topo.die(c) == topo.die(src)][:2]
    far = [c for c in ok if topo.die(c) != topo.die(src)][:2]
    return near + far


def _chunk_relay(rel, c):
    return rel[c % 2]


def _pieces(n):
    q = n // 4
    return [(k * q, (k + 1) * q) for k in range(4)]


def relay_program(g, core, src, dst, T, topo):
    rel = _relays(src, dst, topo)
    k = rel.index(core)
    rid, pid = topo.addr(dst, core)
    m = topo.mask(core, dst)
    n = len(topo.engines(core, dst))
    full = len(topo.engines(src, core))
    sent = [0]

    def pass_on(ap, sem, count):
        g.wait_ge(T.sem[sem], count)
        g.remote_dma(ap, ap, T.sem[sem], T.sem.sent, pid, rid, m)
        sent[0] += n

    a, b = _pieces(64)[k]
    pass_on(T.wn16[:, a:b], "lsa", full // 4)
    for h in range(3):
        a, b = _pieces(W)[k]
        pass_on(T["tab%d" % (h + 1)][:, a:b], "tb%d" % h, full // 4)
        if h == 0 and k == 3:
            pass_on(T.wn16[:, 64:192], "lsb", full)
        if not topo.may_write(src, dst):
            for c, (lo, hi) in enumerate(CH):
                if _chunk_relay(rel, c) == core:
                    pass_on(T.nbi[:, h * TK + lo:h * TK + hi], "ck%d_%d" % (h, c), full)
    g.wait_ge(T.sem.sent, sent[0])


def _spans(o):
    out = []
    for acc, wr in ((o["reads"], False), (o["writes"], True)):
        for name, lo, hi in acc:
            if SCRATCH[name][0] == "psum":
                out.append((name, lo // 512 * 512, -(-hi // 512) * 512, True, wr))
            else:
                out.append((name, lo, hi, False, wr))
    return out


def _plan(ops):
    log = {}
    for i, o in enumerate(ops):
        pre = {}
        if o["after"] is not None:
            pre[o["after"]] = o["delay"]
        for name, lo, hi, bank, wr in _spans(o):
            for l2, h2, w2, j in log.get(name, []):
                if l2 < hi and h2 > lo and (w2 or wr or bank):
                    pre[j] = max(pre.get(j, 0.0), 0.0 if ops[j]["q"] == o["q"] == "pe" else ops[j]["lat"])
        for name, lo, hi, bank, wr in _spans(o):
            log.setdefault(name, []).append((lo, hi, wr, i))
        o["pre"] = pre
    order = list(ORDER) or list(range(len(ops)))
    place = {i: k for k, i in enumerate(order)}
    assert sorted(order) == list(range(len(ops)))
    assert all(place[j] < place[i] for i, o in enumerate(ops) for j in o["pre"])
    return order


def rank_program(g, core, T, topo):
    cores = list(T.cores)
    n_r = len(cores)
    rank = T.rank_of(core)
    if rank is None:
        for r in range(n_r):
            src, dst = cores[r], cores[(r - 1) % n_r]
            if core in topo.cores_of(src) and core in _relays(src, dst, topo):
                relay_program(g, core, src, dst, T, topo)
        return
    dst = cores[(rank - 1) % n_r]
    up = cores[(rank + 1) % n_r]
    rel = _relays(core, dst, topo)
    direct = topo.may_write(core, dst)
    n_in = len(topo.engines(_relays(up, core, topo)[0], core))
    on_chip = topo.engines(core, rel[0])
    V, S, P = g.vector, g.scalar, g.tensor
    cy = EST["cy"]
    ops = []
    sent = [0]

    def add(kind, q, fn, reads, writes, cost, lat, sem=None, val=0, after=None, delay=0.0):
        ops.append({"kind": kind, "q": q, "fn": fn, "reads": reads, "writes": writes, "cost": cost, "lat": lat,
                    "sem": sem, "val": val, "after": after, "delay": delay})
        return len(ops) - 1

    def op(q, fn, reads, writes, cycles):
        return add("op", q, fn, reads, writes, EST["fix"] + max(64, cycles) * cy, EST["sem"])

    def dma(q, sem, out, in_, reads, writes, lat):
        eng = S if q == "act" else g.sync
        return add("dma", q, lambda: eng.dma_start(out, in_), reads, writes, EST["fix"], lat, sem, 16)

    def arrival(sem, val, writes, after, delay):
        add("in", "link", None, [], writes, 0.0, 0.0, sem, val, after, delay)

    def send4(src_t, dst_t, n, sem, reads):
        def fn():
            tr = []
            for k, (a, b) in enumerate(_pieces(n)):
                rid, pid = topo.addr(rel[k], core)
                tr.append(RemoteDMATransfer(dst_ids=[DstId(rid=rid, pnc=pid)],
                                            dma_engine_mask=_mask(on_chip[[0, 2, 1, 3][k]::4]),
                                            remote_sem=T.sem[sem], src=src_t[:, a:b], dst=dst_t[:, a:b]))
            g.remote_dma_fused(tr, local_sem=T.sem.sent)
        sent[0] += len(on_chip)
        return add("out", "pool", fn, reads, [], EST["call"], 0.0)

    def send1(to, out, in_, sem, reads):
        rid, pid = topo.addr(to, core)
        sent[0] += len(topo.engines(core, to))
        return add("out", "pool", lambda: g.remote_dma(out, in_, T.sem[sem], T.sem.sent, pid, rid, topo.mask(core, to)),
                   reads, [], EST["call"], 0.0)

    def whole(name):
        return (name, 0, 128)

    def mm(out, lhs, rhs, start, stop, reads, writes, cycles):
        add("op", "pe", lambda: P.matmul(out, lhs, rhs, start, stop), reads, writes,
            0.03 + max(64, cycles) * EST["pe"], EST["sem"])

    def ts(out, in0, s1, s2, o0, o1, reads, writes, cycles=128):
        if o1 is None:
            op("dve", lambda: V.tensor_scalar(out, in0, s1, None, o0), reads, writes, cycles)
        else:
            op("dve", lambda: V.tensor_scalar(out, in0, s1, s2, o0, o1), reads, writes, cycles)

    def tt(out, in0, in1, o, reads, writes, cycles=256):
        op("dve", lambda: V.tensor_tensor(out, in0, in1, o), reads, writes, cycles)

    def act(out, in_, f, reads, writes, cycles, **kw):
        op("act", lambda: S.activation(out, in_, f, **kw), reads, writes, cycles)

    dma("sp", "wla", T.wl32[:, 0:64], T.wl[:, 0:64], [], [("wl32", 0, 64)], 2.2)
    dma("act", "dla", T.dl32[:, 0:64], T.dl[:, 0:64], [], [("dl32", 0, 64)], 2.2)
    dma("sp", "za", T.z8[:, 0:TK], T.zo[:, 0:TK], [], [("z8", 0, TK)], 2.4)
    dma("act", "wtl", T.wts[:], T.wt[:], [], [("wts", 0, 4)], 2.6)
    dma("act", "ndl", T.ndb[:], T.nd[:], [], [("ndb", 0, D)], 4.0)
    dma("sp", "va", T.v8[:, 0:TK], T.dr[:, 0:TK], [], [("v8", 0, TK)], 2.8)
    dma("sp", "nwl", T.tab0[:], T.nw[:], [], [("tab0", 0, W)], 5.0)
    dma("sp", "wlb", T.wl32[:, 64:256], T.wl[:, 64:256], [], [("wl32", 64, 256)], 6.0)
    dma("sp", "dlb", T.dl32[:, 64:256], T.dl[:, 64:256], [], [("dl32", 64, 256)], 6.5)
    dma("sp", "zb", T.z8[:, TK:], T.zo[:, TK:], [], [("z8", TK, 4 * TK)], 7.0)
    dma("sp", "vb", T.v8[:, TK:], T.dr[:, TK:], [], [("v8", TK, 4 * TK)], 7.0)

    fl = {"allow_small_or_imprecise_dtypes": True}
    op("pool", lambda: g.iota(T.pci[:], [[0, 1]], 0, 1), [], [("pci", 0, 1)], 64)
    op("pool", lambda: g.iota(T.pcf[:], [[0, 1]], 0, 1, **fl), [], [("pcf", 0, 1)], 64)
    op("pool", lambda: g.iota(T.gm[:], [[1, 8], [0, 16]], 0, 0, **fl), [], [whole("gm")], 320)
    op("pool", lambda: g.iota(T.rr[:], [[1, 128]], 0, -1, **fl), [], [whole("rr")], 320)
    op("dve", lambda: V.memset(T.um[:], 0.0), [], [("um", 0, 144)], 64)
    ts(T.gii[:, 0:1], T.pci[:], 4, None, ALU.arith_shift_right, None, [("pci", 0, 1)], [("gii", 0, 1)], 64)
    ts(T.gii[:, 1:2], T.pci[:], 15, None, ALU.bitwise_and, None, [("pci", 0, 1)], [("gii", 1, 2)], 64)
    ts(T.em[:], T.gm[0:8, :], T.pcf[0:8, :], None, ALU.is_equal, None, [whole("gm"), ("pcf", 0, 1)], [whole("em")])
    op("dve", lambda: V.tensor_copy(T.gif[:], T.gii[:]), [("gii", 0, 2)], [("gif", 0, 2)], 64)
    gcol, icol, gi = T.gif[:, 0:1], T.gif[:, 1:2], ("gif", 0, 2)
    ts(T.idm[:], T.rr[:], 0.0, None, ALU.is_equal, None, [whole("rr")], [whole("idm")])
    ts(T.nbd[:], T.gm[:], gcol, -1.0, ALU.is_equal, ALU.mult, [whole("gm"), gi], [whole("nbd")])
    ts(T.t1[:], T.rr[:], 0.0, -32.0, ALU.is_ge, ALU.mult, [whole("rr")], [whole("t1")])
    ts(T.col[:, 0:1], icol, 0.0, 0.5, ALU.is_equal, ALU.mult, [gi], [("col", 0, 1)], 64)
    tt(T.m1[:], T.idm[:], T.nbd[:], ALU.add, [whole("idm"), whole("nbd")], [whole("m1")])
    tt(T.l32[:], T.t1[:], T.nbd[:], ALU.mult, [whole("t1"), whole("nbd")], [whole("l32")])
    act(T.col[:, 2:3], T.col[:, 0:1], ACT.Silu, [("col", 0, 1)], [("col", 2, 3)], 1300, bias=K - 16.0)
    ts(T.t2[:], T.rr[:], 1.0, 0.5, ALU.is_equal, ALU.mult, [whole("rr")], [whole("t2")])
    ts(T.t3[:], T.rr[:], 0.0, 0.5, ALU.is_equal, ALU.mult, [whole("rr")], [whole("t3")])
    tt(T.t2[:], T.t2[:], T.nbd[:], ALU.mult, [whole("t2"), whole("nbd")], [whole("t2")])
    ts(T.um[:, 15:143:16], T.gm[:, 0:128:16], gcol, -0.5, ALU.is_equal, ALU.mult,
       [whole("gm"), gi, ("um", 0, 144)], [("um", 0, 144)], 64)
    tt(T.dm[:], T.t2[:], T.t3[:], ALU.add, [whole("t2"), whole("t3")], [whole("dm")])
    ts(T.col[:, 1:2], T.col[:, 0:1], -1.0, None, ALU.add, None, [("col", 0, 1)], [("col", 1, 2)], 64)
    ts(T.col[:, 3:4], icol, 15.0, None, ALU.is_equal, None, [gi], [("col", 3, 4)], 64)
    ts(T.t4[:], T.nbd[:], T.col[:, 3:4], None, ALU.mult, None, [whole("nbd"), ("col", 3, 4)], [whole("t4")])
    ts(T.t4[:, 0:128:16], T.t4[:, 0:128:16], 0.5, None, ALU.mult, None, [whole("t4")], [whole("t4")], 64)
    tt(T.dm2[:], T.t4[:], T.dm[:], ALU.add, [whole("t4"), whole("dm")], [whole("dm2")])
    bias_b, bias_a = T.col[:, 1:2], T.col[:, 2:3]

    def lists(nm, a, b):
        op("dve", lambda: V.tensor_copy(T[nm + "16"][:, a:b], T[nm + "32"][:, a:b]),
           [(nm + "32", a, b)], [(nm + "16", a, b)], b - a)

    def weights(h):
        a, b = 128 * h, 128 * h + 128
        sc = T.wts[:, h:h + 1]
        act(T.lw[:, a:b], T.l32[:], ACT.Identity, [whole("l32"), ("wts", 0, 4)], [("lw", a, b)], 128, scale=sc)
        act(T.jw[:, a:b], T.nbd[:], ACT.Identity, [whole("nbd"), ("wts", 0, 4)], [("jw", a, b)], 128, scale=sc)

    halves = [(0, 512), (512, TK)]

    def part(name, h, a, b):
        return T[name][:, h * TK + a:h * TK + b], (name, h * TK + a, h * TK + b)

    def off(name, h, a, b):
        lo, hi = (h * TK + a) // 16, (h * TK + b) // 16
        return T[name][:, lo:hi], (name, lo, hi)

    def spread(name, h, a, b):
        src, reg = part(name, h, a, b)
        mm(T.pv[:, a:b], T.em[:], src, True, True, [whole("em"), reg], [("pv", a, b)], b - a)

    def prepare(h):
        for a, b in halves:
            spread("z8", h, a, b)
            ts(T.ne[:, a:b], T.pv[:, a:b], icol, None, ALU.not_equal, None, [("pv", a, b), gi], [("ne", a, b)], b - a)
            spread("v8", h, a, b)
        name, bias = ("ndb", 15.0) if h == 0 else ("at", 15.0 - K)
        for a, b in halves:
            lst, lr = off("dl16", h, a, b)
            act(T.xg[:, a:b], T[name][:, 0:D].indirect(lst), ACT.Identity, [(name, 0, D), lr], [("xg", a, b)],
                (b - a) * EST["g"], bias=bias)
            mm(T.px[:, a:b], T.m1[:], T.ne[:, a:b], True, False, [whole("m1"), ("ne", a, b)], [("px", a, b)], b - a)
            mm(T.px[:, a:b], T.idm[:], T.xg[:, a:b], False, True, [whole("idm"), ("xg", a, b)], [("px", a, b)], b - a)

    def draw(h, c):
        a, b = CH[c]
        n, tab, q, lw = b - a, "tab%d" % h, "pq%d" % (c % 2), (128 * h, 128 * h + 128)
        lst, lr = off("wl16", h, a, b)
        sg, sgr = part("sg", h, a, b)
        tt(T.yb[:, a:b], T[tab][:, 0:W].indirect(lst), T.ne[:, a:b], ALU.add,
           [(tab, 0, W), lr, ("ne", a, b)], [("yb", a, b)], n * EST["g"])
        tt(T.ww[:, a:b], T.px[:, a:b], T.yb[:, a:b], ALU.mult, [("px", a, b), ("yb", a, b)], [("ww", a, b)], n)
        tt(T.wv[:, a:b], T.pv[:, a:b], T.ww[:, a:b], ALU.mult, [("pv", a, b), ("ww", a, b)], [("wv", a, b)], n)
        mm(T[q][:, 0:n], T.lw[:, lw[0]:lw[1]], T.ww[:, a:b], True, False, [("lw",) + lw, ("ww", a, b)],
           [(q, 0, 512)], 4 * n)
        mm(T[q][:, 0:n], T.jw[:, lw[0]:lw[1]], T.wv[:, a:b], False, True, [("jw",) + lw, ("wv", a, b)],
           [(q, 0, 512)], 4 * n)
        act(sg, T[q][:, 0:n], ACT.Sign, [(q, 0, 512)], [sgr], n, bias=-0.5)

    def new_words(h, c):
        a, b = CH[c]
        n, ps, reg = b - a, T.pn0[:, 0:b - a], ("pn0", 0, 512)
        sg, sgr = part("sg", h, a, b)
        out, outr = part("nbo", h, a, b)
        if c in (NBV if h < H - 1 else NBL):
            mm(ps, T.dm2[:], sg, True, True, [whole("dm2"), sgr], [reg], n)
            tt(out, ps, T.yb[:, a:b], ALU.add, [reg, ("yb", a, b)], [outr], n)
        else:
            mm(ps, T.idm[:], T.yb[:, a:b], True, False, [whole("idm"), ("yb", a, b)], [reg], n)
            mm(ps, T.dm[:], sg, False, True, [whole("dm"), sgr], [reg], n)
            act(out, ps, ACT.Identity, [reg, ("col", 1, 2)], [outr], n, bias=bias_b)
        if h < H - 1:
            sem = "ck%d_%d" % (h, c)
            land, lr = part("nbi", h, a, b)
            arrival(sem, n_in, [lr], send1(dst if direct else _chunk_relay(rel, c), land, out, sem, [outr]),
                    EST["chunk"])

    def new_docs(h, a, b):
        sg, sgr = part("sg", h, a, b)
        src, reg = T.pa[:, 0:b - a], ("pa", 0, 512)
        mm(src, T.idm[:], T.xg[:, a:b], True, False, [whole("idm"), ("xg", a, b)], [reg], b - a)
        mm(src, T.idm[:], T.ne[:, a:b], False, False, [("ne", a, b)], [reg], b - a)
        mm(src, T.dm[:], sg, False, True, [whole("dm"), sgr], [reg], b - a)
        act(T.na[:, a:b], src, ACT.Identity, [reg, ("col", 2, 3)], [("na", a, b)], b - a, bias=bias_a)
        for lo in range(a, b, DOC):
            hi = min(b, lo + DOC)
            lst, lr = off("dl16", h, lo, hi)
            act(T.at[:, 0:D].indirect(lst), T.na[:, lo:hi], ACT.Silu, [("na", lo, hi), lr], [("at", 0, D)],
                (hi - lo) * EST["s"])

    def scatter_word(h, c):
        a, b = CH[c]
        tab, lst, src = ("tab%d" % (h + 1), "wn16", "nbi") if h < H - 1 else ("tab3", "wl16", "nbo")
        lst, lr = off(lst, h, a, b)
        src, sr = part(src, h, a, b)
        op("dve", lambda: V.tensor_copy(T[tab][:, 0:W].indirect(lst), src), [sr, lr], [(tab, 0, W)], (b - a) * EST["s"])

    def topics(ps, name, slots):
        for t in slots:
            mm(ps[:, 0:256], T.um[:, 15 - t:143 - t], T.sg[:, 256 * t:256 * t + 256], t == slots[0], t == slots[-1],
               [("um", 0, 144), ("sg", 256 * t, 256 * t + 256)], [(name, 0, 256)], 256)

    lists("wl", 0, 64)
    lists("dl", 0, 64)
    arrival("lsa", 4 * n_in, [("wn16", 0, 64)], send4(T.wl16, T.wn16, 64, "lsa", [("wl16", 0, 64)]), EST["table"])
    lists("wl", 64, 256)
    lists("dl", 64, 256)
    for h in range(H):
        weights(h)
    for a in range(0, D, 320):
        act(T.at[:, a:a + 320], T.ndb[:, a:a + 320], ACT.Identity, [("ndb", a, a + 320)], [("at", a, a + 320)], 320,
            bias=K)

    for h in range(H):
        prepare(h)
        if h < H - 1:
            i = send4(T["tab%d" % h], T["tab%d" % (h + 1)], W, "tb%d" % h, [("tab%d" % h, 0, W)])
            arrival("tb%d" % h, 4 * n_in, [("tab%d" % (h + 1), 0, W)], i, EST["table"])
        if h == 0:
            i = send1(rel[3], T.wn16[:, 64:192], T.wl16[:, 64:192], "lsb", [("wl16", 64, 192), ("tab0", 0, W)])
            arrival("lsb", n_in, [("wn16", 64, 192)], i, EST["table"])
        for c in range(NC):
            draw(h, c)
            new_words(h, c)
        for a, b in DOCP:
            new_docs(h, a, b)
        for c in range(NC):
            scatter_word(h, c)
        if h == H - 2:
            topics(T.pq1, "pq1", range(12))
            ts(T.zc[:], T.pq1[:, 0:256], 8.0, None, ALU.add, None, [("pq1", 0, 256)], [("zc", 0, 256)], 256)

    topics(T.pv, "pv", range(12, 16))
    tt(T.zc[:], T.pv[:, 0:256], T.zc[:], ALU.add, [("pv", 0, 256), ("zc", 0, 256)], [("zc", 0, 256)], 256)
    dma("pool2", "oyz", T.yz[:], T.zc[:], [("zc", 0, 256)], [], 2.0)
    dma("pool2", "oyw", T.yw[:], T.tab3[:], [("tab3", 0, W)], [], 3.0)
    act(T.ndb[:, 0:CUT], T.at[:, 0:CUT], ACT.Relu, [("at", 0, CUT)], [("ndb", 0, CUT)], CUT, bias=-(K + 0.001))
    dma("act", "oyd0", T.yd[:, 0:CUT], T.ndb[:, 0:CUT], [("ndb", 0, CUT)], [], 2.5)
    ts(T.ndb[:, CUT:D], T.at[:, CUT:D], -(K + 0.001), 0.0, ALU.add, ALU.max, [("at", CUT, D)], [("ndb", CUT, D)],
       D - CUT)
    dma("pool2", "oyd1", T.yd[:, CUT:D], T.ndb[:, CUT:D], [("ndb", CUT, D)], [], 2.5)

    queue = {"pe": P, "act": S, "dve": V, "pool": g, "sp": g.sync}
    count = {"pe": 0, "act": 0, "dve": 0, "pool": 0}
    known = {q: {} for q in queue}
    log, top, waited = {}, {}, {}
    for i in _plan(ops):
        o = ops[i]
        q = "sp" if o["q"] == "pool2" else o["q"]
        if o["kind"] != "in":
            toks = []
            for name, lo, hi, bank, wr in _spans(o):
                for l2, h2, w2, tok, clk in log.get(name, []):
                    if l2 < hi and h2 > lo and (w2 or wr or (bank and tok[0] != q)) and not tok[0] == q == "pe":
                        toks.append((tok, clk))
            toks.sort(key=lambda t: -t[0][1])
            for (sem, val), clk in toks:
                if known[q].get(sem, 0) >= val:
                    continue
                queue[q].wait_ge(T.sem[sem], val)
                waited[sem] = max(waited.get(sem, 0), val)
                known[q][sem] = val
                for s2, v2 in clk.items():
                    if known[q].get(s2, 0) < v2:
                        known[q][s2] = v2
        if o["kind"] == "out":
            o["fn"]()
            continue
        if o["kind"] == "op":
            count[q] += 1
            tok = (q, count[q])
            o["fn"]().then_inc(T.sem[q], 1)
        else:
            tok = (o["sem"], o["val"])
            if o["kind"] == "dma":
                o["fn"]().then_inc(T.sem[o["sem"]], 16)
        clk = {} if o["kind"] == "in" else dict(known[q])
        top[tok[0]] = max(top.get(tok[0], 0), tok[1])
        for name, lo, hi, bank, wr in _spans(o):
            log.setdefault(name, []).append((lo, hi, wr, tok, clk))

    g.wait_ge(T.sem.sent, sent[0])
    for sem, val in top.items():
        if waited.get(sem, 0) < val:
            g.wait_ge(T.sem[sem], val)
